import numpy as np
import ml_dtypes


def mxq(x, axis, fmt="e4m3"):
    dtype, down = {"e4m3": (ml_dtypes.float8_e4m3fn, 7), "e5m2": (ml_dtypes.float8_e5m2, 14)}[fmt]
    v = np.moveaxis(np.asarray(x, np.float32).astype(ml_dtypes.bfloat16).astype(np.float64), axis, -1)
    blocks = v.reshape(v.shape[:-1] + (-1, 32))
    amax = np.abs(blocks).max(-1, keepdims=True)
    byte = np.maximum(np.where(amax > 0, np.frexp(amax)[1] - 1 + 127, 0) - down, 1)
    scale = np.exp2(byte - 127.0)
    codes = (blocks / scale).astype(np.float32).astype(dtype).astype(np.float64)
    return np.moveaxis((codes * scale).reshape(v.shape), -1, axis)


WIDE = False


def mx_kscale(k):
    if not WIDE:
        return np.ones(k)
    levels = np.array([10, -10, 5, -5, 0])
    if k % 512:
        return np.exp2(np.random.permutation(np.resize(levels, k // 32))).repeat(32)
    a = np.empty((k // 512, 16))
    for p in range(k // 512):
        a[p, :8] = np.random.permutation(np.resize(levels, 8))
        for g in range(8):
            far = levels[np.abs(levels - a[p, g]) >= 10]
            a[p, g + 8] = far[np.random.randint(len(far))]
    return np.exp2(a.ravel()).repeat(32)


def f64(x):
    return np.asarray(x).astype(np.float64)


def striped(idx):
    return np.tile(idx.reshape(-1, 16).T, (8, 1)).astype(np.uint16)


def unstriped(offs):
    return offs[:16].T.reshape(-1).astype(np.int64)


def striped8(idx):
    return np.concatenate([x.reshape(-1, 16).T for x in idx]).astype(np.uint16)


def runs(offs, k):
    lists = np.stack([offs[16 * r : 16 * r + 16].T.reshape(-1) for r in range(8)]).astype(np.int64)
    return lists[np.arange(k) % 512 // 64]


def pack_weight(w):
    k, n = w.shape
    w = f64(np.asarray(w, np.float32).astype(ml_dtypes.bfloat16)).reshape(k // 32, 32, n)
    amax = np.abs(w).max(1)
    byte = np.clip(np.where(amax > 0, np.frexp(amax)[1] - 1 + 127 - 7, 1), 1, 254)
    scaled = (w * np.exp2(127.0 - byte)[:, None, :]).reshape(k, n).astype(np.float32)
    words = np.ascontiguousarray(scaled.reshape(k // 512, 128, 4, n).transpose(0, 1, 3, 2)).astype(ml_dtypes.float8_e4m3fn).view(np.uint8)
    return words, np.ascontiguousarray(byte.astype(np.uint8).reshape(k // 512, 16, n))


def unpack_weight(words, scales):
    g, p, n, _ = words.shape
    vals = np.ascontiguousarray(words).view(ml_dtypes.float8_e4m3fn).astype(np.float64) * np.repeat(np.exp2(scales.astype(np.float64) - 127.0), 8, axis=1)[..., None]
    return vals.transpose(0, 1, 3, 2).reshape(g * 512, n)


def sigmoid(v):
    return 1.0 / (1.0 + np.exp(-np.maximum(v, -700.0)))


K, T, S, H, C = 512, 2048, 512, 512, 512


def setup_inputs():
    n = np.random.standard_normal
    s = mx_kscale(K)[:, None]
    packed_xT = pack_weight(n((K, T)) * s)
    return {
        "x_words": packed_xT[0],
        "x_scales": packed_xT[1],
        "w1": (n((K, H)) / np.sqrt(K) / s).astype(np.float32),
        "w2": (n((K, H)) / np.sqrt(K) / s).astype(np.float32),
        "gs": (np.random.uniform(0.5, 1.5, (K, 1)) / s).astype(np.float32),
        "offs": striped(np.random.permutation(T)[:S]),
        "two": striped(np.random.permutation(T)[:S]),
        "n1": striped8(np.stack([np.random.permutation(S) for _ in range(8)])),
        "n2": striped8(np.stack([np.random.permutation(S) for _ in range(8)])),
        "cand": striped(np.random.permutation(T)[:C]),
        "n3": striped8(np.stack([np.random.permutation(S) for _ in range(8)])),
        "n4": striped8(np.stack([np.random.permutation(S) for _ in range(8)])),
    }


def reference(x_words, x_scales, w1, w2, gs, offs, two, n1, n2, cand, n3, n4):
    x_cand = unpack_weight(x_words, x_scales)[:, unstriped(cand)]
    xq = unpack_weight(x_words, x_scales)[:, unstriped(offs)]
    y = mxq(f64(w1), 0, "e4m3").T @ xq
    x_two = unpack_weight(x_words, x_scales)[:, unstriped(two)]
    d = mxq(f64(w2), 0, "e4m3").T @ x_two
    z = f64(gs) * (y * (sigmoid(d[np.arange(H)[:, None], runs(n2, H)])) - (0.5 * (y[np.arange(H)[:, None], runs(n1, H)])))
    s = 0.0625 * ((x_cand.T @ mxq(z, 0, "e4m3")))
    return (np.tanh(s[np.arange(C)[:, None], runs(n3, C)] - s)) * (s[np.arange(C)[:, None], runs(n4, C)])

@@ -1,0 +1,183 @@
+import concourse.mybir as mybir
+
+F32 = mybir.dt.float32
+BF16 = mybir.dt.bfloat16
+I32 = mybir.dt.int32
+U32 = mybir.dt.uint32
+U16 = mybir.dt.uint16
+U8 = mybir.dt.uint8
+FP8X4 = mybir.dt.float8_e4m3fn_x4
+ACT = mybir.ActivationFunctionType
+ALU = mybir.AluOpType
+
+P, K, T, S, H, C = 128, 512, 2048, 512, 512, 512
+PACK = 4
+HALF = S // 2
+FLOPS = 3 * 2 * 512 * 512 * 512
+GATE_ON_SCALAR = (True, True, True, True)
+
+
+def tile_picked_twcgatebfdif_none_p_kernel(tc, x_words, x_scales, w1, w2, gs, offs, two, n1, n2, cand, n3, n4, out):
+    nc = tc.nc
+    with (
+        tc.tile_pool(name="keep", bufs=1) as keep,
+        tc.psum_pool(name="psum", bufs=1) as psum,
+    ):
+        def load_list(src, name):
+            tile = keep.tile([P, S // 16], U16, name=name)
+            nc.sync.dma_start(tile[:], src)
+            return tile
+
+        def half_of(lst, h):
+            return lst[:, h * (HALF // 16):(h + 1) * (HALF // 16)]
+
+        def load_weight(w, name):
+            halves = []
+            rows = w.rearrange("(p j) c -> p j c", j=PACK)
+            for h in range(2):
+                raw = keep.tile([P, PACK, H // 2], F32, name=f"{name}_raw{h}")
+                nc.sync.dma_start(raw[:], rows[:, :, h * (H // 2):(h + 1) * (H // 2)])
+                halves.append(raw)
+            return halves
+
+        def weave(engine_copy, grouped, raw, h):
+            dst = grouped[:].rearrange("p (t m j) -> p m j t", t=PACK, j=PACK)[:, h * 64:(h + 1) * 64]
+            engine_copy(dst, raw[:].rearrange("p j (m t) -> p m j t", t=PACK))
+
+        def quantise(grouped, name):
+            codes = keep.tile([P, 512], U32, name=f"{name}_codes", align_bytes=64)
+            scales = keep.tile([P, 512], U8, name=f"{name}_scales", align_bytes=64)
+            nc.vector.quantize_mx(out=codes[:].bitcast(FP8X4), scales=scales[:], in_=grouped[:])
+            return codes, scales
+
+        def pick(window, lst, dtype, name):
+            picked = keep.tile([P, S], dtype, name=name, align_bytes=64)
+            nc.vector.tensor_copy(picked[:], window.indirect(lst[:]))
+            return picked
+
+        def product(bank, lhs, t, rhs, cols):
+            m = slice(t * P, (t + 1) * P)
+            nc.tensor.matmul_mx(out=bank, lhsT=lhs[0][:, m].bitcast(FP8X4), lhsT_scale=lhs[1][:, m],
+                                rhs=rhs[0][:, cols].bitcast(FP8X4), rhs_scale=rhs[1][:, cols], start=True, stop=True)
+
+        warm = keep.tile([P, 8], F32, name="warm")
+        xs = keep.tile([P, T], U8, name="xs")
+        nc.vector.memset(xs[:].bitcast(I32), 0)
+        nc.gpsimd.memset(warm[:], 0.0)
+        nc.scalar.activation(warm[:], warm[:], ACT.Sigmoid)
+        two_l = load_list(two, "two_l")
+        offs_l = load_list(offs, "offs_l")
+        cand_l = load_list(cand, "cand_l")
+        for q in range(4):
+            nc.sync.dma_start(xs[32 * q:32 * q + 4, :].bitcast(I32), x_scales[0, 4 * q:4 * q + 4, :].bitcast(I32))
+        w2_raw = load_weight(w2, "w2")
+        xw = keep.tile([P, T], I32, name="xw")
+        nc.sync.dma_start(xw[:], x_words[0].rearrange("p n r -> p (n r)").bitcast(I32))
+        n2_l = load_list(n2, "n2_l")
+        gain = keep.tile([P, PACK], F32, name="gain")
+        nc.sync.dma_start(gain[:], gs.rearrange("(p t) o -> p (t o)", t=PACK))
+        w1_raw = load_weight(w1, "w1")
+        n1_l = load_list(n1, "n1_l")
+        n3_l = load_list(n3, "n3_l")
+        n4_l = load_list(n4, "n4_l")
+
+        two_s = pick(xs[:], two_l, U8, "two_s")
+        offs_s = pick(xs[:], offs_l, U8, "offs_s")
+        cand_s = pick(xs[:], cand_l, U8, "cand_s")
+
+        w2_g = keep.tile([P, H * PACK], BF16, name="w2_g", align_bytes=64)
+        for h in range(2):
+            weave(nc.scalar.copy, w2_g, w2_raw[h], h)
+        w2_q = quantise(w2_g, "w2")
+        words = xw[:].bitcast(U32)
+        two_w = pick(words, two_l, U32, "two_w")
+        offs_w = pick(words, offs_l, U32, "offs_w")
+
+        d_banks = [psum.tile([P, S], F32, name=f"bank{t}") for t in range(PACK)]
+        for t in range(PACK):
+            product(d_banks[t][:], w2_q, t, (two_w, two_s), slice(0, S))
+
+        gain2 = keep.tile([P, PACK], F32, name="gain2")
+        nc.vector.tensor_scalar_mul(gain2[:], gain[:], 2.0)
+
+        w1_g = keep.tile([P, H * PACK], BF16, name="w1_g", align_bytes=64)
+        for h in range(2):
+            weave(nc.vector.tensor_copy, w1_g, w1_raw[h], h)
+        w1_q = quantise(w1_g, "w1")
+        y_banks = [psum.tile([P, S], F32, name=f"bank{PACK + t}") for t in range(PACK)]
+        for t in range(PACK):
+            product(y_banks[t][:], w1_q, t, (offs_w, offs_s), slice(0, S))
+
+        cand_w = pick(words, cand_l, U32, "cand_w")
+        cand_wd = keep.tile([P, C], U32, name="cand_wd", align_bytes=64)
+        cand_sd = keep.tile([P, C], U8, name="cand_sd", align_bytes=64)
+        nc.vector.tensor_copy(cand_wd[:].rearrange("p (t m) -> p t m", t=PACK), cand_w[:].rearrange("p (m t) -> p t m", t=PACK))
+        nc.vector.tensor_copy(cand_sd[:].rearrange("p (t m) -> p t m", t=PACK), cand_s[:].rearrange("p (m t) -> p t m", t=PACK))
+
+        d_sb = [keep.tile([P, S], F32, name=f"d_sb{t}") for t in range(PACK)]
+        y_sb = [keep.tile([P, S], F32, name=f"y_sb{t}") for t in range(PACK)]
+        y2_sb = [keep.tile([P, S], F32, name=f"y2_sb{t}") for t in range(PACK)]
+        gate = [keep.tile([P, S], F32, name=f"gate{t}") for t in range(PACK)]
+        gated = [keep.tile([P, S], F32, name=f"gated{t}") for t in range(PACK)]
+        u = [keep.tile([P, PACK, HALF], F32, name=f"u{h}") for h in range(2)]
+        z_codes = keep.tile([P, S], U32, name="z_codes", align_bytes=64)
+        z_scales = keep.tile([P, S], U8, name="z_scales", align_bytes=64)
+        z_g = keep.tile([P, S * PACK], BF16, name="z_g", align_bytes=64)
+
+        for h in range(2):
+            cols = slice(h * HALF, (h + 1) * HALF)
+            for t in range(PACK):
+                if h == 0:
+                    if GATE_ON_SCALAR[t]:
+                        nc.scalar.copy(d_sb[t][:], d_banks[t][:])
+                    else:
+                        nc.scalar.activation(d_sb[t][:], d_banks[t][:], ACT.Sigmoid)
+                if GATE_ON_SCALAR[t]:
+                    nc.scalar.activation(gate[t][:, cols], d_sb[t][:].indirect(half_of(n2_l, h)), ACT.Sigmoid)
+                if h == 0:
+                    nc.scalar.activation(y_sb[t][:], y_banks[t][:], ACT.Copy, scale=gain[:, t:t + 1])
+                    if not GATE_ON_SCALAR[t]:
+                        nc.scalar.activation(y2_sb[t][:], y_banks[t][:], ACT.Copy, scale=gain2[:, t:t + 1])
+                if GATE_ON_SCALAR[t]:
+                    nc.vector.scalar_tensor_tensor(gated[t][:, cols], y_sb[t][:, cols], 2.0, gate[t][:, cols], ALU.mult, ALU.mult)
+                else:
+                    nc.vector.tensor_tensor(gated[t][:, cols], d_sb[t][:].indirect(half_of(n2_l, h)), y2_sb[t][:, cols], ALU.mult)
+            for t in range(PACK):
+                nc.vector.tensor_tensor(u[h][:, t, :], y_sb[t][:].indirect(half_of(n1_l, h)), gated[t][:, cols], ALU.subtract)
+            wide = slice(h * HALF * PACK, (h + 1) * HALF * PACK)
+            nc.scalar.activation(z_g[:, wide].rearrange("p (c i t) -> p c t i", i=4, t=PACK),
+                                 u[h][:].rearrange("p t (c i) -> p c t i", i=4), ACT.Copy, scale=-0.5)
+            nc.vector.quantize_mx(out=z_codes[:, cols].bitcast(FP8X4), scales=z_scales[:, cols], in_=z_g[:, wide])
+
+        s_banks = [psum.tile([P, S], F32, name=f"bank{t}") for t in range(PACK)]
+        for t in range(PACK):
+            for h in range(2):
+                cols = slice(h * HALF, (h + 1) * HALF)
+                product(s_banks[t][:, cols], (cand_wd, cand_sd), t, (z_codes, z_scales), cols)
+
+        s_a = [keep.tile([P, S], F32, name=f"s_a{t}") for t in range(PACK)]
+        s_b = [keep.tile([P, S], F32, name=f"s_b{t}") for t in range(PACK)]
+        diff = [keep.tile([P, S], F32, name=f"diff{t}") for t in range(PACK)]
+        bent = [keep.tile([P, S], F32, name=f"bent{t}") for t in range(PACK)]
+        res = [keep.tile([P, S], F32, name=f"res{t}") for t in range(PACK)]
+        out_rows = out.rearrange("(p t) j -> t p j", t=PACK)
+
+        def first(t):
+            nc.scalar.activation(s_a[t][:], s_banks[t][:], ACT.Copy, scale=0.0625)
+            nc.scalar.activation(s_b[t][:], s_banks[t][:], ACT.Copy, scale=0.0625)
+            for h in range(2):
+                cols = slice(h * HALF, (h + 1) * HALF)
+                nc.vector.tensor_tensor(diff[t][:, cols], s_a[t][:].indirect(half_of(n3_l, h)), s_b[t][:, cols], ALU.subtract)
+                nc.scalar.activation(bent[t][:, cols], diff[t][:, cols], ACT.Tanh)
+
+        def second(t):
+            for h in range(2):
+                cols = slice(h * HALF, (h + 1) * HALF)
+                nc.vector.tensor_tensor(res[t][:, cols], s_a[t][:].indirect(half_of(n4_l, h)), bent[t][:, cols], ALU.mult)
+                nc.sync.dma_start(out_rows[t][:, cols], res[t][:, cols])
+
+        first(0)
+        for t in range(1, PACK):
+            first(t)
+            second(t - 1)
+        second(PACK - 1)

@@ -13,14 +13,15 @@ ALU = mybir.AluOpType
 P, K, T, S, H, C = 128, 512, 2048, 512, 512, 512
 PACK = 4
 HALF = S // 2
+RUNS = 8
 FLOPS = 3 * 2 * 512 * 512 * 512
-GATE_ON_SCALAR = (True, True, True, True)
 
 
 def tile_picked_twcgatebfdif_none_p_kernel(tc, x_words, x_scales, w1, w2, gs, offs, two, n1, n2, cand, n3, n4, out):
     nc = tc.nc
     with (
         tc.tile_pool(name="keep", bufs=1) as keep,
+        tc.tile_pool(name="reused", bufs=1) as reused,
         tc.psum_pool(name="psum", bufs=1) as psum,
     ):
         def load_list(src, name):
@@ -28,21 +29,18 @@ def tile_picked_twcgatebfdif_none_p_kernel(tc, x_words, x_scales, w1, w2, gs, of
             nc.sync.dma_start(tile[:], src)
             return tile
 
-        def half_of(lst, h):
-            return lst[:, h * (HALF // 16):(h + 1) * (HALF // 16)]
+        def part(lst, cols):
+            return lst[:, cols.start // 16:cols.stop // 16]
 
-        def load_weight(w, name):
-            halves = []
-            rows = w.rearrange("(p j) c -> p j c", j=PACK)
-            for h in range(2):
-                raw = keep.tile([P, PACK, H // 2], F32, name=f"{name}_raw{h}")
-                nc.sync.dma_start(raw[:], rows[:, :, h * (H // 2):(h + 1) * (H // 2)])
-                halves.append(raw)
-            return halves
+        def load_weight_half(w, h, name):
+            raw = keep.tile([P, PACK * H // 2], F32, name=name, align_bytes=64)
+            nc.sync.dma_start(raw[:].rearrange("p (j c) -> p j c", j=PACK),
+                              w.rearrange("(p j) c -> p j c", j=PACK)[:, :, h * (H // 2):(h + 1) * (H // 2)])
+            return raw
 
         def weave(engine_copy, grouped, raw, h):
             dst = grouped[:].rearrange("p (t m j) -> p m j t", t=PACK, j=PACK)[:, h * 64:(h + 1) * 64]
-            engine_copy(dst, raw[:].rearrange("p j (m t) -> p m j t", t=PACK))
+            engine_copy(dst, raw[:].rearrange("p (j m t) -> p m j t", j=PACK, t=PACK))
 
         def quantise(grouped, name):
             codes = keep.tile([P, 512], U32, name=f"{name}_codes", align_bytes=64)
@@ -50,8 +48,7 @@ def tile_picked_twcgatebfdif_none_p_kernel(tc, x_words, x_scales, w1, w2, gs, of
             nc.vector.quantize_mx(out=codes[:].bitcast(FP8X4), scales=scales[:], in_=grouped[:])
             return codes, scales
 
-        def pick(window, lst, dtype, name):
-            picked = keep.tile([P, S], dtype, name=name, align_bytes=64)
+        def pick(window, lst, picked):
             nc.vector.tensor_copy(picked[:], window.indirect(lst[:]))
             return picked
 
@@ -67,117 +64,155 @@ def tile_picked_twcgatebfdif_none_p_kernel(tc, x_words, x_scales, w1, w2, gs, of
         nc.scalar.activation(warm[:], warm[:], ACT.Sigmoid)
         two_l = load_list(two, "two_l")
         offs_l = load_list(offs, "offs_l")
-        cand_l = load_list(cand, "cand_l")
+        w2_raw = [load_weight_half(w2, 0, "w2_raw0")]
         for q in range(4):
             nc.sync.dma_start(xs[32 * q:32 * q + 4, :].bitcast(I32), x_scales[0, 4 * q:4 * q + 4, :].bitcast(I32))
-        w2_raw = load_weight(w2, "w2")
+        w2_raw.append(load_weight_half(w2, 1, "w2_raw1"))
         xw = keep.tile([P, T], I32, name="xw")
         nc.sync.dma_start(xw[:], x_words[0].rearrange("p n r -> p (n r)").bitcast(I32))
-        n2_l = load_list(n2, "n2_l")
         gain = keep.tile([P, PACK], F32, name="gain")
         nc.sync.dma_start(gain[:], gs.rearrange("(p t) o -> p (t o)", t=PACK))
-        w1_raw = load_weight(w1, "w1")
+        n2_l = load_list(n2, "n2_l")
+        w1_raw = [load_weight_half(w1, h, f"w1_raw{h}") for h in range(2)]
+        cand_l = load_list(cand, "cand_l")
         n1_l = load_list(n1, "n1_l")
         n3_l = load_list(n3, "n3_l")
         n4_l = load_list(n4, "n4_l")
 
-        two_s = pick(xs[:], two_l, U8, "two_s")
-        offs_s = pick(xs[:], offs_l, U8, "offs_s")
-        cand_s = pick(xs[:], cand_l, U8, "cand_s")
-
+        words = xw[:].bitcast(U32)
+        two_s = pick(xs[:], two_l, keep.tile([P, S], U8, name="two_s", align_bytes=64))
+        offs_s = pick(xs[:], offs_l, keep.tile([P, S], U8, name="offs_s", align_bytes=64))
         w2_g = keep.tile([P, H * PACK], BF16, name="w2_g", align_bytes=64)
         for h in range(2):
             weave(nc.scalar.copy, w2_g, w2_raw[h], h)
         w2_q = quantise(w2_g, "w2")
-        words = xw[:].bitcast(U32)
-        two_w = pick(words, two_l, U32, "two_w")
-        offs_w = pick(words, offs_l, U32, "offs_w")
+        two_w = pick(words, two_l, keep.tile([P, S], U32, name="two_w", align_bytes=64))
+        offs_w = pick(words, offs_l, keep.tile([P, S], U32, name="offs_w", align_bytes=64))
+        everything = slice(0, S)
+        d_banks, y_banks = {}, {}
 
-        d_banks = [psum.tile([P, S], F32, name=f"bank{t}") for t in range(PACK)]
-        for t in range(PACK):
-            product(d_banks[t][:], w2_q, t, (two_w, two_s), slice(0, S))
+        def d_product(t, bank):
+            d_banks[t] = psum.tile([P, S], F32, name=f"d_bank{t}", tag=f"bank{bank}")
+            product(d_banks[t][:], w2_q, t, (two_w, two_s), everything)
 
-        gain2 = keep.tile([P, PACK], F32, name="gain2")
-        nc.vector.tensor_scalar_mul(gain2[:], gain[:], 2.0)
+        def y_product(t, bank):
+            y_banks[t] = psum.tile([P, S], F32, name=f"y_bank{t}", tag=f"bank{bank}")
+            product(y_banks[t][:], w1_q, t, (offs_w, offs_s), everything)
 
-        w1_g = keep.tile([P, H * PACK], BF16, name="w1_g", align_bytes=64)
+        d_product(0, 0)
+        d_product(1, 1)
+
+        w1_g = reused.tile([P, H * PACK], BF16, name="w1_g", align_bytes=64, offset=0)
         for h in range(2):
             weave(nc.vector.tensor_copy, w1_g, w1_raw[h], h)
         w1_q = quantise(w1_g, "w1")
-        y_banks = [psum.tile([P, S], F32, name=f"bank{PACK + t}") for t in range(PACK)]
-        for t in range(PACK):
-            product(y_banks[t][:], w1_q, t, (offs_w, offs_s), slice(0, S))
-
-        cand_w = pick(words, cand_l, U32, "cand_w")
+        y_product(0, 2)
+        y_product(1, 3)
+        cand_s = pick(xs[:], cand_l, reused.tile([P, C], U8, name="cand_s", align_bytes=64, offset=0))
+        cand_w = pick(words, cand_l, reused.tile([P, C], U32, name="cand_w", align_bytes=64, offset=C))
         cand_wd = keep.tile([P, C], U32, name="cand_wd", align_bytes=64)
         cand_sd = keep.tile([P, C], U8, name="cand_sd", align_bytes=64)
-        nc.vector.tensor_copy(cand_wd[:].rearrange("p (t m) -> p t m", t=PACK), cand_w[:].rearrange("p (m t) -> p t m", t=PACK))
-        nc.vector.tensor_copy(cand_sd[:].rearrange("p (t m) -> p t m", t=PACK), cand_s[:].rearrange("p (m t) -> p t m", t=PACK))
+        for dealt, picked in ((cand_sd, cand_s), (cand_wd, cand_w)):
+            for t in range(PACK):
+                nc.sync.dma_start(dealt[:, t * P:(t + 1) * P].bitcast(I32).rearrange("p (r w) -> p r w", r=RUNS),
+                                  picked[:].bitcast(I32).rearrange("p (r t w) -> p t r w", r=RUNS, t=PACK)[:, t])
+        wide_s = w2_raw + w1_raw
 
-        d_sb = [keep.tile([P, S], F32, name=f"d_sb{t}") for t in range(PACK)]
+        halves = [slice(0, HALF), slice(HALF, S)]
+        gate_sb = [keep.tile([P, S], F32, name=f"gate_sb{t}") for t in range(PACK)]
         y_sb = [keep.tile([P, S], F32, name=f"y_sb{t}") for t in range(PACK)]
-        y2_sb = [keep.tile([P, S], F32, name=f"y2_sb{t}") for t in range(PACK)]
-        gate = [keep.tile([P, S], F32, name=f"gate{t}") for t in range(PACK)]
-        gated = [keep.tile([P, S], F32, name=f"gated{t}") for t in range(PACK)]
-        u = [keep.tile([P, PACK, HALF], F32, name=f"u{h}") for h in range(2)]
+        raw_z = [keep.tile([P, PACK, HALF], F32, name=f"raw_z{h}") for h in range(2)]
+        gated = [[wide_s[t][:, S + h * HALF:S + (h + 1) * HALF] for h in range(2)] for t in range(PACK)]
+        gated[3][0] = raw_z[1][:, 2, :]
         z_codes = keep.tile([P, S], U32, name="z_codes", align_bytes=64)
         z_scales = keep.tile([P, S], U8, name="z_scales", align_bytes=64)
-        z_g = keep.tile([P, S * PACK], BF16, name="z_g", align_bytes=64)
+        z_g = [keep.tile([P, HALF * PACK], BF16, name=f"z_g{h}", align_bytes=64) for h in range(2)]
 
-        for h in range(2):
-            cols = slice(h * HALF, (h + 1) * HALF)
-            for t in range(PACK):
-                if h == 0:
-                    if GATE_ON_SCALAR[t]:
-                        nc.scalar.copy(d_sb[t][:], d_banks[t][:])
-                    else:
-                        nc.scalar.activation(d_sb[t][:], d_banks[t][:], ACT.Sigmoid)
-                if GATE_ON_SCALAR[t]:
-                    nc.scalar.activation(gate[t][:, cols], d_sb[t][:].indirect(half_of(n2_l, h)), ACT.Sigmoid)
-                if h == 0:
-                    nc.scalar.activation(y_sb[t][:], y_banks[t][:], ACT.Copy, scale=gain[:, t:t + 1])
-                    if not GATE_ON_SCALAR[t]:
-                        nc.scalar.activation(y2_sb[t][:], y_banks[t][:], ACT.Copy, scale=gain2[:, t:t + 1])
-                if GATE_ON_SCALAR[t]:
-                    nc.vector.scalar_tensor_tensor(gated[t][:, cols], y_sb[t][:, cols], 2.0, gate[t][:, cols], ALU.mult, ALU.mult)
-                else:
-                    nc.vector.tensor_tensor(gated[t][:, cols], d_sb[t][:].indirect(half_of(n2_l, h)), y2_sb[t][:, cols], ALU.mult)
-            for t in range(PACK):
-                nc.vector.tensor_tensor(u[h][:, t, :], y_sb[t][:].indirect(half_of(n1_l, h)), gated[t][:, cols], ALU.subtract)
-            wide = slice(h * HALF * PACK, (h + 1) * HALF * PACK)
-            nc.scalar.activation(z_g[:, wide].rearrange("p (c i t) -> p c t i", i=4, t=PACK),
-                                 u[h][:].rearrange("p t (c i) -> p c t i", i=4), ACT.Copy, scale=-0.5)
-            nc.vector.quantize_mx(out=z_codes[:, cols].bitcast(FP8X4), scales=z_scales[:, cols], in_=z_g[:, wide])
+        def d_out(t):
+            nc.scalar.copy(wide_s[t][:, :S], d_banks[t][:])
 
-        s_banks = [psum.tile([P, S], F32, name=f"bank{t}") for t in range(PACK)]
-        for t in range(PACK):
+        def y_out(t):
+            nc.scalar.activation(y_sb[t][:], y_banks[t][:], ACT.Copy, scale=gain[:, t:t + 1])
+
+        def gate(t):
+            nc.scalar.activation(gate_sb[t][:], wide_s[t][:].indirect(n2_l[:]), ACT.Sigmoid)
+
+        def times_gate(t, h):
+            cols = halves[h]
+            nc.vector.scalar_tensor_tensor(gated[t][h], y_sb[t][:, cols], 2.0, gate_sb[t][:, cols], ALU.mult, ALU.mult)
+
+        def less_neighbour(t, h):
+            nc.vector.tensor_tensor(raw_z[h][:, t, :], y_sb[t][:].indirect(part(n1_l, halves[h])), gated[t][h], ALU.subtract)
+
+        def z_views(h, lo, hi):
+            return (z_g[h][:, lo * PACK:hi * PACK].rearrange("p (c i t) -> p c t i", i=4, t=PACK),
+                    raw_z[h][:, :, lo:hi].rearrange("p t (c i) -> p c t i", i=4))
+
+        def z_quantise(h):
+            nc.vector.quantize_mx(out=z_codes[:, halves[h]].bitcast(FP8X4), scales=z_scales[:, halves[h]], in_=z_g[h][:])
+
+        def combine(t):
             for h in range(2):
-                cols = slice(h * HALF, (h + 1) * HALF)
-                product(s_banks[t][:, cols], (cand_wd, cand_sd), t, (z_codes, z_scales), cols)
+                times_gate(t, h)
+            for h in range(2):
+                less_neighbour(t, h)
 
-        s_a = [keep.tile([P, S], F32, name=f"s_a{t}") for t in range(PACK)]
+        d_out(0)
+        d_out(1)
+        gate(0)
+        gate(1)
+        y_out(0)
+        d_product(2, 2)
+        y_product(2, 4)
+        y_out(1)
+        d_product(3, 3)
+        y_product(3, 5)
+        combine(0)
+        combine(1)
+        for t in range(2, PACK):
+            d_out(t)
+            y_out(t)
+            gate(t)
+            for h in range(2):
+                times_gate(t, h)
+            less_neighbour(t, 0)
+        for t in range(2, PACK):
+            less_neighbour(t, 1)
+        nc.scalar.activation(*z_views(0, 0, HALF), ACT.Copy, scale=-0.5)
+        nc.scalar.activation(*z_views(1, 0, 128), ACT.Copy, scale=-0.5)
+        z_quantise(0)
+        nc.vector.tensor_scalar_mul(*z_views(1, 128, HALF), -0.5)
+        z_quantise(1)
+
+        cand_q, z_q = (cand_wd, cand_sd), (z_codes, z_scales)
+        s_parts = [[(psum.tile([P, HALF], F32, name=f"s_bank0{h}", tag=f"bank{6 + h}"), halves[h]) for h in range(2)]]
+        for t in range(1, PACK):
+            s_parts.append([(psum.tile([P, S], F32, name=f"s_bank{t}", tag=f"bank{(0, 1, 4)[t - 1]}"), everything)])
+        for t in range(PACK):
+            for bank, cols in s_parts[t]:
+                product(bank[:], cand_q, t, z_q, cols)
+
         s_b = [keep.tile([P, S], F32, name=f"s_b{t}") for t in range(PACK)]
         diff = [keep.tile([P, S], F32, name=f"diff{t}") for t in range(PACK)]
         bent = [keep.tile([P, S], F32, name=f"bent{t}") for t in range(PACK)]
         res = [keep.tile([P, S], F32, name=f"res{t}") for t in range(PACK)]
-        out_rows = out.rearrange("(p t) j -> t p j", t=PACK)
+        out_rows = out.rearrange("(r t q) j -> t r q j", r=RUNS, t=PACK)
 
-        def first(t):
-            nc.scalar.activation(s_a[t][:], s_banks[t][:], ACT.Copy, scale=0.0625)
-            nc.scalar.activation(s_b[t][:], s_banks[t][:], ACT.Copy, scale=0.0625)
-            for h in range(2):
-                cols = slice(h * HALF, (h + 1) * HALF)
-                nc.vector.tensor_tensor(diff[t][:, cols], s_a[t][:].indirect(half_of(n3_l, h)), s_b[t][:, cols], ALU.subtract)
-                nc.scalar.activation(bent[t][:, cols], diff[t][:, cols], ACT.Tanh)
+        def s_out(t):
+            for bank, cols in s_parts[t]:
+                nc.scalar.activation(wide_s[t][:, cols], bank[:], ACT.Copy, scale=0.0625)
+                nc.scalar.activation(s_b[t][:, cols], bank[:], ACT.Copy, scale=0.0625)
+            for cols in (halves if t == 0 else [everything]):
+                nc.vector.tensor_tensor(diff[t][:, cols], wide_s[t][:].indirect(part(n3_l, cols)), s_b[t][:, cols], ALU.subtract)
 
-        def second(t):
-            for h in range(2):
-                cols = slice(h * HALF, (h + 1) * HALF)
-                nc.vector.tensor_tensor(res[t][:, cols], s_a[t][:].indirect(half_of(n4_l, h)), bent[t][:, cols], ALU.mult)
-                nc.sync.dma_start(out_rows[t][:, cols], res[t][:, cols])
+        def finish(t):
+            nc.scalar.activation(bent[t][:], diff[t][:], ACT.Tanh)
+            for cols in (halves if t == PACK - 1 else [everything]):
+                nc.vector.tensor_tensor(res[t][:, cols], wide_s[t][:].indirect(part(n4_l, cols)), bent[t][:, cols], ALU.mult)
+                nc.sync.dma_start(out_rows[t][:, :, cols], res[t][:, cols])
 
-        first(0)
+        s_out(0)
         for t in range(1, PACK):
-            first(t)
-            second(t - 1)
-        second(PACK - 1)
+            s_out(t)
+            finish(t - 1)
+        finish(PACK - 1)

@@ -109,13 +109,11 @@ def tile_picked_twcgatebfdif_none_p_kernel(tc, x_words, x_scales, w1, w2, gs, of
         y_product(0, 2)
         y_product(1, 3)
         cand_s = pick(xs[:], cand_l, reused.tile([P, C], U8, name="cand_s", align_bytes=64, offset=0))
-        cand_w = pick(words, cand_l, reused.tile([P, C], U32, name="cand_w", align_bytes=64, offset=C))
-        cand_wd = keep.tile([P, C], U32, name="cand_wd", align_bytes=64)
+        cand_wd = reused.tile([P, C], U32, name="cand_wd", align_bytes=64, offset=C)
+        nc.vector.tensor_copy(cand_wd[:].rearrange("p (t r q) -> p r t q", t=PACK, r=RUNS), words.indirect(cand_l[:]))
         cand_sd = keep.tile([P, C], U8, name="cand_sd", align_bytes=64)
-        for dealt, picked in ((cand_sd, cand_s), (cand_wd, cand_w)):
-            for t in range(PACK):
-                nc.sync.dma_start(dealt[:, t * P:(t + 1) * P].bitcast(I32).rearrange("p (r w) -> p r w", r=RUNS),
-                                  picked[:].bitcast(I32).rearrange("p (r t w) -> p t r w", r=RUNS, t=PACK)[:, t])
+        nc.vector.tensor_copy(cand_sd[:].bitcast(I32).rearrange("p (t r w) -> p r t w", t=PACK, r=RUNS),
+                              cand_s[:].bitcast(I32).rearrange("p (r t w) -> p r t w", t=PACK, r=RUNS))
         wide_s = w2_raw + w1_raw
 
         halves = [slice(0, HALF), slice(HALF, S)]
@@ -126,7 +124,9 @@ def tile_picked_twcgatebfdif_none_p_kernel(tc, x_words, x_scales, w1, w2, gs, of
         gated[3][0] = raw_z[1][:, 2, :]
         z_codes = keep.tile([P, S], U32, name="z_codes", align_bytes=64)
         z_scales = keep.tile([P, S], U8, name="z_scales", align_bytes=64)
-        z_g = [keep.tile([P, HALF * PACK], BF16, name=f"z_g{h}", align_bytes=64) for h in range(2)]
+        pieces = [slice(0, HALF), slice(HALF, HALF + P), slice(HALF + P, S)]
+        z_g = [reused.tile([P, (c.stop - c.start) * PACK], BF16, name=f"z_g{i}", align_bytes=64, offset=4096 + (0, 2048, 0)[i])
+               for i, c in enumerate(pieces)]
 
         def d_out(t):
             nc.scalar.copy(wide_s[t][:, :S], d_banks[t][:])
@@ -144,12 +144,13 @@ def tile_picked_twcgatebfdif_none_p_kernel(tc, x_words, x_scales, w1, w2, gs, of
         def less_neighbour(t, h):
             nc.vector.tensor_tensor(raw_z[h][:, t, :], y_sb[t][:].indirect(part(n1_l, halves[h])), gated[t][h], ALU.subtract)
 
-        def z_views(h, lo, hi):
-            return (z_g[h][:, lo * PACK:hi * PACK].rearrange("p (c i t) -> p c t i", i=4, t=PACK),
-                    raw_z[h][:, :, lo:hi].rearrange("p t (c i) -> p c t i", i=4))
+        def z_views(i):
+            h = pieces[i].start // HALF
+            return (z_g[i][:].rearrange("p (c i t) -> p c t i", i=4, t=PACK),
+                    raw_z[h][:, :, pieces[i].start - h * HALF:pieces[i].stop - h * HALF].rearrange("p t (c i) -> p c t i", i=4))
 
-        def z_quantise(h):
-            nc.vector.quantize_mx(out=z_codes[:, halves[h]].bitcast(FP8X4), scales=z_scales[:, halves[h]], in_=z_g[h][:])
+        def z_quantise(i):
+            nc.vector.quantize_mx(out=z_codes[:, pieces[i]].bitcast(FP8X4), scales=z_scales[:, pieces[i]], in_=z_g[i][:])
 
         def combine(t):
             for h in range(2):
@@ -178,16 +179,17 @@ def tile_picked_twcgatebfdif_none_p_kernel(tc, x_words, x_scales, w1, w2, gs, of
             less_neighbour(t, 0)
         for t in range(2, PACK):
             less_neighbour(t, 1)
-        nc.scalar.activation(*z_views(0, 0, HALF), ACT.Copy, scale=-0.5)
-        nc.scalar.activation(*z_views(1, 0, 128), ACT.Copy, scale=-0.5)
+        nc.scalar.activation(*z_views(0), ACT.Copy, scale=-0.5)
+        nc.scalar.activation(*z_views(1), ACT.Copy, scale=-0.5)
         z_quantise(0)
-        nc.vector.tensor_scalar_mul(*z_views(1, 128, HALF), -0.5)
+        nc.vector.tensor_scalar_mul(*z_views(2), -0.5)
         z_quantise(1)
+        z_quantise(2)
 
         cand_q, z_q = (cand_wd, cand_sd), (z_codes, z_scales)
-        s_parts = [[(psum.tile([P, HALF], F32, name=f"s_bank0{h}", tag=f"bank{6 + h}"), halves[h]) for h in range(2)]]
+        s_parts = [[(psum.tile([P, c.stop - c.start], F32, name=f"s_bank0{i}", tag=f"bank{5 + i}"), c) for i, c in enumerate(pieces)]]
         for t in range(1, PACK):
-            s_parts.append([(psum.tile([P, S], F32, name=f"s_bank{t}", tag=f"bank{(0, 1, 4)[t - 1]}"), everything)])
+            s_parts.append([(psum.tile([P, S], F32, name=f"s_bank{t}", tag=f"bank{t - 1}"), everything)])
         for t in range(PACK):
             for bank, cols in s_parts[t]:
                 product(bank[:], cand_q, t, z_q, cols)
@@ -201,13 +203,17 @@ def tile_picked_twcgatebfdif_none_p_kernel(tc, x_words, x_scales, w1, w2, gs, of
         def s_out(t):
             for bank, cols in s_parts[t]:
                 nc.scalar.activation(wide_s[t][:, cols], bank[:], ACT.Copy, scale=0.0625)
-                nc.scalar.activation(s_b[t][:, cols], bank[:], ACT.Copy, scale=0.0625)
+            for bank, cols in s_parts[t]:
+                if cols == pieces[0]:
+                    nc.vector.tensor_scalar_mul(s_b[t][:, cols], bank[:], 0.0625)
+                else:
+                    nc.scalar.activation(s_b[t][:, cols], bank[:], ACT.Copy, scale=0.0625)
             for cols in (halves if t == 0 else [everything]):
                 nc.vector.tensor_tensor(diff[t][:, cols], wide_s[t][:].indirect(part(n3_l, cols)), s_b[t][:, cols], ALU.subtract)
 
         def finish(t):
             nc.scalar.activation(bent[t][:], diff[t][:], ACT.Tanh)
-            for cols in (halves if t == PACK - 1 else [everything]):
+            for cols in ([slice(0, S - P), slice(S - P, S)] if t == PACK - 1 else [everything]):
                 nc.vector.tensor_tensor(res[t][:, cols], wide_s[t][:].indirect(part(n4_l, cols)), bent[t][:, cols], ALU.mult)
                 nc.sync.dma_start(out_rows[t][:, :, cols], res[t][:, cols])
 

@@ -13,7 +13,7 @@ ALU = mybir.AluOpType
 P, K, T, S, H, C = 128, 512, 2048, 512, 512, 512
 PACK = 4
 HALF = S // 2
-RUNS = 8
+RUNS = 16
 FLOPS = 3 * 2 * 512 * 512 * 512
 
 
@@ -32,19 +32,13 @@ def tile_picked_twcgatebfdif_none_p_kernel(tc, x_words, x_scales, w1, w2, gs, of
         def part(lst, cols):
             return lst[:, cols.start // 16:cols.stop // 16]
 
-        def load_weight_half(w, h, name):
-            raw = keep.tile([P, PACK * H // 2], F32, name=name, align_bytes=64)
-            nc.sync.dma_start(raw[:].rearrange("p (j c) -> p j c", j=PACK),
-                              w.rearrange("(p j) c -> p j c", j=PACK)[:, :, h * (H // 2):(h + 1) * (H // 2)])
-            return raw
-
-        def weave(engine_copy, grouped, raw, h):
-            dst = grouped[:].rearrange("p (t m j) -> p m j t", t=PACK, j=PACK)[:, h * 64:(h + 1) * 64]
-            engine_copy(dst, raw[:].rearrange("p (j m t) -> p m j t", j=PACK, t=PACK))
+        def weave(engine_copy, grouped, raw, u):
+            engine_copy(grouped[:].rearrange("p (t m j) -> p m j t", t=2, j=PACK),
+                        raw[:].rearrange("p (j m t) -> p m j t", j=PACK, t=PACK)[:, :, :, 2 * u:2 * u + 2])
 
         def quantise(grouped, name):
-            codes = keep.tile([P, 512], U32, name=f"{name}_codes", align_bytes=64)
-            scales = keep.tile([P, 512], U8, name=f"{name}_scales", align_bytes=64)
+            codes = keep.tile([P, 2 * P], U32, name=f"{name}_codes", align_bytes=64)
+            scales = keep.tile([P, 2 * P], U8, name=f"{name}_scales", align_bytes=64)
             nc.vector.quantize_mx(out=codes[:].bitcast(FP8X4), scales=scales[:], in_=grouped[:])
             return codes, scales
 
@@ -62,19 +56,25 @@ def tile_picked_twcgatebfdif_none_p_kernel(tc, x_words, x_scales, w1, w2, gs, of
         nc.vector.memset(xs[:].bitcast(I32), 0)
         nc.gpsimd.memset(warm[:], 0.0)
         nc.scalar.activation(warm[:], warm[:], ACT.Sigmoid)
+        zeroed = [keep.tile([P, 2 * S], F32, name=f"zeroed{t}") for t in range(2)]
+        for tile in zeroed:
+            nc.gpsimd.memset(tile[:, S:], 0.0)
         two_l = load_list(two, "two_l")
         offs_l = load_list(offs, "offs_l")
-        w2_raw = [load_weight_half(w2, 0, "w2_raw0")]
+        w2_raw = keep.tile([P, PACK * H], F32, name="w2_raw")
+        w2_rows = w2.rearrange("(p j) c -> p (j c)", j=PACK)
+        nc.sync.dma_start(w2_raw[:, :2 * H], w2_rows[:, :2 * H])
         for q in range(4):
             nc.sync.dma_start(xs[32 * q:32 * q + 4, :].bitcast(I32), x_scales[0, 4 * q:4 * q + 4, :].bitcast(I32))
-        w2_raw.append(load_weight_half(w2, 1, "w2_raw1"))
+        nc.sync.dma_start(w2_raw[:, 2 * H:], w2_rows[:, 2 * H:])
+        cand_l = load_list(cand, "cand_l")
         xw = keep.tile([P, T], I32, name="xw")
         nc.sync.dma_start(xw[:], x_words[0].rearrange("p n r -> p (n r)").bitcast(I32))
         gain = keep.tile([P, PACK], F32, name="gain")
         nc.sync.dma_start(gain[:], gs.rearrange("(p t) o -> p (t o)", t=PACK))
         n2_l = load_list(n2, "n2_l")
-        w1_raw = [load_weight_half(w1, h, f"w1_raw{h}") for h in range(2)]
-        cand_l = load_list(cand, "cand_l")
+        w1_raw = keep.tile([P, PACK * H], F32, name="w1_raw")
+        nc.sync.dma_start(w1_raw[:], w1.rearrange("(p j) c -> p (j c)", j=PACK))
         n1_l = load_list(n1, "n1_l")
         n3_l = load_list(n3, "n3_l")
         n4_l = load_list(n4, "n4_l")
@@ -82,10 +82,11 @@ def tile_picked_twcgatebfdif_none_p_kernel(tc, x_words, x_scales, w1, w2, gs, of
         words = xw[:].bitcast(U32)
         two_s = pick(xs[:], two_l, keep.tile([P, S], U8, name="two_s", align_bytes=64))
         offs_s = pick(xs[:], offs_l, keep.tile([P, S], U8, name="offs_s", align_bytes=64))
-        w2_g = keep.tile([P, H * PACK], BF16, name="w2_g", align_bytes=64)
-        for h in range(2):
-            weave(nc.scalar.copy, w2_g, w2_raw[h], h)
-        w2_q = quantise(w2_g, "w2")
+        cand_s = pick(xs[:], cand_l, keep.tile([P, C], U8, name="cand_s", align_bytes=64))
+        w2_g = [keep.tile([P, 2 * H], BF16, name=f"w2_g{u}", align_bytes=64) for u in range(2)]
+        for u in range(2):
+            weave(nc.scalar.copy, w2_g[u], w2_raw, u)
+        w2_q = [quantise(w2_g[0], "w2_q")]
         two_w = pick(words, two_l, keep.tile([P, S], U32, name="two_w", align_bytes=64))
         offs_w = pick(words, offs_l, keep.tile([P, S], U32, name="offs_w", align_bytes=64))
         everything = slice(0, S)
@@ -93,28 +94,28 @@ def tile_picked_twcgatebfdif_none_p_kernel(tc, x_words, x_scales, w1, w2, gs, of
 
         def d_product(t, bank):
             d_banks[t] = psum.tile([P, S], F32, name=f"d_bank{t}", tag=f"bank{bank}")
-            product(d_banks[t][:], w2_q, t, (two_w, two_s), everything)
+            product(d_banks[t][:], w2_q[t // 2], t % 2, (two_w, two_s), everything)
 
         def y_product(t, bank):
             y_banks[t] = psum.tile([P, S], F32, name=f"y_bank{t}", tag=f"bank{bank}")
-            product(y_banks[t][:], w1_q, t, (offs_w, offs_s), everything)
+            product(y_banks[t][:], w1_q[t // 2], t % 2, (offs_w, offs_s), everything)
 
         d_product(0, 0)
         d_product(1, 1)
+        w2_q.append(quantise(w2_g[1], "w2_q"))
 
-        w1_g = reused.tile([P, H * PACK], BF16, name="w1_g", align_bytes=64, offset=0)
-        for h in range(2):
-            weave(nc.vector.tensor_copy, w1_g, w1_raw[h], h)
-        w1_q = quantise(w1_g, "w1")
+        w1_g = [reused.tile([P, 2 * H], BF16, name=f"w1_g{u}", align_bytes=64, offset=2048 * u) for u in range(2)]
+        for u in range(2):
+            weave(nc.vector.tensor_copy, w1_g[u], w1_raw, u)
+        w1_q = [quantise(w1_g[u], f"w1_q{u}") for u in range(2)]
         y_product(0, 2)
         y_product(1, 3)
-        cand_s = pick(xs[:], cand_l, reused.tile([P, C], U8, name="cand_s", align_bytes=64, offset=0))
-        cand_wd = reused.tile([P, C], U32, name="cand_wd", align_bytes=64, offset=C)
+        cand_wd = reused.tile([P, C], U32, name="cand_wd", align_bytes=64, offset=2048)
         nc.vector.tensor_copy(cand_wd[:].rearrange("p (t r q) -> p r t q", t=PACK, r=RUNS), words.indirect(cand_l[:]))
-        cand_sd = keep.tile([P, C], U8, name="cand_sd", align_bytes=64)
+        cand_sd = reused.tile([P, C], U8, name="cand_sd", align_bytes=64, offset=0)
         nc.vector.tensor_copy(cand_sd[:].bitcast(I32).rearrange("p (t r w) -> p r t w", t=PACK, r=RUNS),
                               cand_s[:].bitcast(I32).rearrange("p (r t w) -> p r t w", t=PACK, r=RUNS))
-        wide_s = w2_raw + w1_raw
+        wide_s = zeroed + [w2_raw, w1_raw]
 
         halves = [slice(0, HALF), slice(HALF, S)]
         gate_sb = [keep.tile([P, S], F32, name=f"gate_sb{t}") for t in range(PACK)]

@@ -10,11 +10,26 @@ FP8X4 = mybir.dt.float8_e4m3fn_x4
 ACT = mybir.ActivationFunctionType
 ALU = mybir.AluOpType
 
-P, K, T, S, H, C = 128, 512, 2048, 512, 512, 512
+P = 128
+T = 2048
+S = 512
+H = 512
+C = 512
 PACK = 4
+TILES = 4
+PAIR = 2
 HALF = S // 2
-RUNS = 16
+LIST_ROWS = 16
+CAND_GROUPS = 16
+LINE = 4
+ALIGN = 64
 FLOPS = 3 * 2 * 512 * 512 * 512
+
+W1_WOVEN_AT = (0, 2048)
+W2_CODES_AT, W2_SCALES_AT, CAND_DEALT_AT, CAND_BYTES_AT = 0, 1024, 1280, 1792
+CAND_WORDS_AT = 2048
+MINUS_Z_AT = (4096, 8192)
+Z_WOVEN_AT = (12288, 14336, MINUS_Z_AT[0])
 
 
 def tile_picked_twcgatebfdif_none_p_kernel(tc, x_words, x_scales, w1, w2, gs, offs, two, n1, n2, cand, n3, n4, out):
@@ -25,40 +40,43 @@ def tile_picked_twcgatebfdif_none_p_kernel(tc, x_words, x_scales, w1, w2, gs, of
         tc.psum_pool(name="psum", bufs=1) as psum,
     ):
         def load_list(src, name):
-            tile = keep.tile([P, S // 16], U16, name=name)
+            tile = keep.tile([P, S // LIST_ROWS], U16, name=name)
             nc.sync.dma_start(tile[:], src)
             return tile
 
-        def part(lst, cols):
-            return lst[:, cols.start // 16:cols.stop // 16]
+        def entries(lst, cols):
+            return lst[:, cols.start // LIST_ROWS:cols.stop // LIST_ROWS]
 
-        def weave(engine_copy, grouped, raw, u):
-            engine_copy(grouped[:].rearrange("p (t m j) -> p m j t", t=2, j=PACK),
-                        raw[:].rearrange("p (j m t) -> p m j t", j=PACK, t=PACK)[:, :, :, 2 * u:2 * u + 2])
+        def weave(engine_copy, woven, raw, u):
+            engine_copy(woven[:].rearrange("p (t m j) -> p m j t", t=PAIR, j=PACK),
+                        raw[:].rearrange("p (j m t) -> p m j t", j=PACK, t=TILES)[:, :, :, PAIR * u:PAIR * (u + 1)])
 
-        def quantise(grouped, name):
-            codes = keep.tile([P, 2 * P], U32, name=f"{name}_codes", align_bytes=64)
-            scales = keep.tile([P, 2 * P], U8, name=f"{name}_scales", align_bytes=64)
-            nc.vector.quantize_mx(out=codes[:].bitcast(FP8X4), scales=scales[:], in_=grouped[:])
+        def quantise(woven, codes, scales):
+            nc.vector.quantize_mx(out=codes[:].bitcast(FP8X4), scales=scales[:], in_=woven[:])
             return codes, scales
 
-        def pick(window, lst, picked):
-            nc.vector.tensor_copy(picked[:], window.indirect(lst[:]))
+        def weight_tiles(name):
+            return (keep.tile([P, PAIR * P], U32, name=f"{name}_codes", align_bytes=ALIGN),
+                    keep.tile([P, PAIR * P], U8, name=f"{name}_scales", align_bytes=ALIGN))
+
+        def pick(window, offsets, picked):
+            nc.vector.tensor_copy(picked[:], window.indirect(offsets))
             return picked
 
-        def product(bank, lhs, t, rhs, cols):
-            m = slice(t * P, (t + 1) * P)
+        def product(bank, lhs, block, rhs, cols):
+            m = slice(block * P, (block + 1) * P)
             nc.tensor.matmul_mx(out=bank, lhsT=lhs[0][:, m].bitcast(FP8X4), lhsT_scale=lhs[1][:, m],
                                 rhs=rhs[0][:, cols].bitcast(FP8X4), rhs_scale=rhs[1][:, cols], start=True, stop=True)
 
-        warm = keep.tile([P, 8], F32, name="warm")
         xs = keep.tile([P, T], U8, name="xs")
         nc.vector.memset(xs[:].bitcast(I32), 0)
-        nc.gpsimd.memset(warm[:], 0.0)
-        nc.scalar.activation(warm[:], warm[:], ACT.Sigmoid)
-        zeroed = [keep.tile([P, 2 * S], F32, name=f"zeroed{t}") for t in range(2)]
-        for tile in zeroed:
+        one_half = keep.tile([P, 8], F32, name="one_half")
+        nc.gpsimd.memset(one_half[:], 0.0)
+        nc.scalar.activation(one_half[:], one_half[:], ACT.Sigmoid)
+        cleared = [keep.tile([P, 2 * S], F32, name=f"cleared{t}") for t in range(PAIR)]
+        for tile in cleared:
             nc.gpsimd.memset(tile[:, S:], 0.0)
+
         two_l = load_list(two, "two_l")
         offs_l = load_list(offs, "offs_l")
         w2_raw = keep.tile([P, PACK * H], F32, name="w2_raw")
@@ -70,8 +88,8 @@ def tile_picked_twcgatebfdif_none_p_kernel(tc, x_words, x_scales, w1, w2, gs, of
         cand_l = load_list(cand, "cand_l")
         xw = keep.tile([P, T], I32, name="xw")
         nc.sync.dma_start(xw[:], x_words[0].rearrange("p n r -> p (n r)").bitcast(I32))
-        gain = keep.tile([P, PACK], F32, name="gain")
-        nc.sync.dma_start(gain[:], gs.rearrange("(p t) o -> p (t o)", t=PACK))
+        gain = keep.tile([P, TILES], F32, name="gain")
+        nc.sync.dma_start(gain[:], gs.rearrange("(p t) o -> p (t o)", t=TILES))
         n2_l = load_list(n2, "n2_l")
         w1_raw = keep.tile([P, PACK * H], F32, name="w1_raw")
         nc.sync.dma_start(w1_raw[:], w1.rearrange("(p j) c -> p (j c)", j=PACK))
@@ -79,147 +97,154 @@ def tile_picked_twcgatebfdif_none_p_kernel(tc, x_words, x_scales, w1, w2, gs, of
         n3_l = load_list(n3, "n3_l")
         n4_l = load_list(n4, "n4_l")
 
-        words = xw[:].bitcast(U32)
-        two_s = pick(xs[:], two_l, keep.tile([P, S], U8, name="two_s", align_bytes=64))
-        offs_s = pick(xs[:], offs_l, keep.tile([P, S], U8, name="offs_s", align_bytes=64))
-        cand_s = pick(xs[:], cand_l, keep.tile([P, C], U8, name="cand_s", align_bytes=64))
-        w2_g = [keep.tile([P, 2 * H], BF16, name=f"w2_g{u}", align_bytes=64) for u in range(2)]
-        for u in range(2):
-            weave(nc.scalar.copy, w2_g[u], w2_raw, u)
-        w2_q = [quantise(w2_g[0], "w2_q")]
-        two_w = pick(words, two_l, keep.tile([P, S], U32, name="two_w", align_bytes=64))
-        offs_w = pick(words, offs_l, keep.tile([P, S], U32, name="offs_w", align_bytes=64))
+        halves = [slice(0, HALF), slice(HALF, S)]
         everything = slice(0, S)
+        words = xw[:].bitcast(U32)
+        two_s = pick(xs[:], two_l[:], keep.tile([P, S], U8, name="two_s", align_bytes=ALIGN))
+        offs_s = pick(xs[:], offs_l[:], keep.tile([P, S], U8, name="offs_s", align_bytes=ALIGN))
+        cand_s = [pick(xs[:], entries(cand_l, halves[0]), keep.tile([P, C // 2], U8, name="cand_s0", align_bytes=ALIGN))]
+        w2_woven = [keep.tile([P, PAIR * P * PACK], BF16, name=f"w2_woven{u}", align_bytes=ALIGN) for u in range(2)]
+        for u in range(2):
+            weave(nc.scalar.copy, w2_woven[u], w2_raw, u)
+        w2_q = [quantise(w2_woven[0], *weight_tiles("w2_q0"))]
+        two_w = pick(words, two_l[:], keep.tile([P, S], U32, name="two_w", align_bytes=ALIGN))
+        offs_w = pick(words, offs_l[:], keep.tile([P, S], U32, name="offs_w", align_bytes=ALIGN))
+        half_gain = keep.tile([P, TILES], F32, name="half_gain")
+        nc.scalar.activation(half_gain[:], gain[:], ACT.Copy, scale=one_half[:, 0:1])
+
         d_banks, y_banks = {}, {}
 
         def d_product(t, bank):
             d_banks[t] = psum.tile([P, S], F32, name=f"d_bank{t}", tag=f"bank{bank}")
-            product(d_banks[t][:], w2_q[t // 2], t % 2, (two_w, two_s), everything)
+            product(d_banks[t][:], w2_q[t // PAIR], t % PAIR, (two_w, two_s), everything)
 
         def y_product(t, bank):
             y_banks[t] = psum.tile([P, S], F32, name=f"y_bank{t}", tag=f"bank{bank}")
-            product(y_banks[t][:], w1_q[t // 2], t % 2, (offs_w, offs_s), everything)
+            product(y_banks[t][:], w1_q[t // PAIR], t % PAIR, (offs_w, offs_s), everything)
 
-        d_product(0, 0)
-        d_product(1, 1)
-        w2_q.append(quantise(w2_g[1], "w2_q"))
+        d_product(0, bank=0)
+        d_product(1, bank=1)
 
-        w1_g = [reused.tile([P, 2 * H], BF16, name=f"w1_g{u}", align_bytes=64, offset=2048 * u) for u in range(2)]
+        w1_woven = [reused.tile([P, PAIR * P * PACK], BF16, name=f"w1_woven{u}", align_bytes=ALIGN, offset=W1_WOVEN_AT[u])
+                    for u in range(2)]
         for u in range(2):
-            weave(nc.vector.tensor_copy, w1_g[u], w1_raw, u)
-        w1_q = [quantise(w1_g[u], f"w1_q{u}") for u in range(2)]
-        y_product(0, 2)
-        y_product(1, 3)
-        cand_wd = reused.tile([P, C], U32, name="cand_wd", align_bytes=64, offset=2048)
-        nc.vector.tensor_copy(cand_wd[:].rearrange("p (t r q) -> p r t q", t=PACK, r=RUNS), words.indirect(cand_l[:]))
-        cand_sd = reused.tile([P, C], U8, name="cand_sd", align_bytes=64, offset=0)
-        nc.vector.tensor_copy(cand_sd[:].bitcast(I32).rearrange("p (t r w) -> p r t w", t=PACK, r=RUNS),
-                              cand_s[:].bitcast(I32).rearrange("p (r t w) -> p r t w", t=PACK, r=RUNS))
-        wide_s = zeroed + [w2_raw, w1_raw]
+            weave(nc.vector.tensor_copy, w1_woven[u], w1_raw, u)
+        w1_q = [quantise(w1_woven[u], *weight_tiles(f"w1_q{u}")) for u in range(2)]
+        y_product(0, bank=2)
+        y_product(1, bank=3)
 
-        halves = [slice(0, HALF), slice(HALF, S)]
-        gate_sb = [keep.tile([P, S], F32, name=f"gate_sb{t}") for t in range(PACK)]
-        y_sb = [keep.tile([P, S], F32, name=f"y_sb{t}") for t in range(PACK)]
-        raw_z = [keep.tile([P, PACK, HALF], F32, name=f"raw_z{h}") for h in range(2)]
-        gated = [[wide_s[t][:, S + h * HALF:S + (h + 1) * HALF] for h in range(2)] for t in range(PACK)]
-        gated[3][0] = raw_z[1][:, 2, :]
-        z_codes = keep.tile([P, S], U32, name="z_codes", align_bytes=64)
-        z_scales = keep.tile([P, S], U8, name="z_scales", align_bytes=64)
-        pieces = [slice(0, HALF), slice(HALF, HALF + P), slice(HALF + P, S)]
-        z_g = [reused.tile([P, (c.stop - c.start) * PACK], BF16, name=f"z_g{i}", align_bytes=64, offset=4096 + (0, 2048, 0)[i])
-               for i, c in enumerate(pieces)]
+        w2_q.append(quantise(w2_woven[1],
+                             reused.tile([P, PAIR * P], U32, name="w2_q1_codes", align_bytes=ALIGN, offset=W2_CODES_AT),
+                             reused.tile([P, PAIR * P], U8, name="w2_q1_scales", align_bytes=ALIGN, offset=W2_SCALES_AT)))
+        cand_s.append(pick(xs[:], entries(cand_l, halves[1]),
+                           reused.tile([P, C // 2], U8, name="cand_s1", align_bytes=ALIGN, offset=CAND_BYTES_AT)))
+        cand_words = reused.tile([P, C], U32, name="cand_words", align_bytes=ALIGN, offset=CAND_WORDS_AT)
+        nc.vector.tensor_copy(cand_words[:].rearrange("p (t a b) -> p a t b", t=TILES, a=CAND_GROUPS), words.indirect(cand_l[:]))
+        cand_scales = reused.tile([P, C], U8, name="cand_scales", align_bytes=ALIGN, offset=CAND_DEALT_AT)
+        dealt = cand_scales[:].bitcast(I32).rearrange("p (t a w) -> p a t w", t=TILES, a=CAND_GROUPS)
+        for h in range(2):
+            nc.vector.tensor_copy(dealt[:, h * CAND_GROUPS // 2:(h + 1) * CAND_GROUPS // 2],
+                                  cand_s[h][:].bitcast(I32).rearrange("p (a t w) -> p a t w", t=TILES, a=CAND_GROUPS // 2))
+
+        windows = cleared + [w2_raw, w1_raw]
+        gate = [keep.tile([P, S], F32, name=f"gate{t}") for t in range(TILES)]
+        half_y = [keep.tile([P, S], F32, name=f"half_y{t}") for t in range(TILES)]
+        minus_z = [reused.tile([P, TILES, HALF], F32, name=f"minus_z{h}", align_bytes=ALIGN, offset=MINUS_Z_AT[h])
+                   for h in range(2)]
+        gated = [[windows[t][:, S + h * HALF:S + (h + 1) * HALF] for h in range(2)] for t in range(TILES)]
+        gated[3][0] = minus_z[1][:, 2, :]
+        z_codes = keep.tile([P, S], U32, name="z_codes", align_bytes=ALIGN)
+        z_scales = keep.tile([P, S], U8, name="z_scales", align_bytes=ALIGN)
+        pieces = [halves[0], slice(HALF, HALF + P), slice(HALF + P, S)]
+        z_woven = [reused.tile([P, (c.stop - c.start) * PACK], BF16, name=f"z_woven{i}", align_bytes=ALIGN, offset=Z_WOVEN_AT[i])
+                   for i, c in enumerate(pieces)]
 
         def d_out(t):
-            nc.scalar.copy(wide_s[t][:, :S], d_banks[t][:])
+            nc.scalar.copy(windows[t][:, :S], d_banks[t][:])
 
         def y_out(t):
-            nc.scalar.activation(y_sb[t][:], y_banks[t][:], ACT.Copy, scale=gain[:, t:t + 1])
+            nc.scalar.activation(half_y[t][:], y_banks[t][:], ACT.Copy, scale=half_gain[:, t:t + 1])
 
-        def gate(t):
-            nc.scalar.activation(gate_sb[t][:], wide_s[t][:].indirect(n2_l[:]), ACT.Sigmoid)
+        def fetch_gate(t):
+            nc.scalar.activation(gate[t][:], windows[t][:].indirect(n2_l[:]), ACT.Sigmoid)
 
         def times_gate(t, h):
-            cols = halves[h]
-            nc.vector.scalar_tensor_tensor(gated[t][h], y_sb[t][:, cols], 2.0, gate_sb[t][:, cols], ALU.mult, ALU.mult)
+            nc.vector.scalar_tensor_tensor(gated[t][h], half_y[t][:, halves[h]], 2.0, gate[t][:, halves[h]], ALU.mult, ALU.mult)
 
-        def less_neighbour(t, h):
-            nc.vector.tensor_tensor(raw_z[h][:, t, :], y_sb[t][:].indirect(part(n1_l, halves[h])), gated[t][h], ALU.subtract)
+        def neighbour_less_gated(t, h):
+            nc.vector.tensor_tensor(minus_z[h][:, t, :], half_y[t][:].indirect(entries(n1_l, halves[h])), gated[t][h], ALU.subtract)
 
         def z_views(i):
             h = pieces[i].start // HALF
-            return (z_g[i][:].rearrange("p (c i t) -> p c t i", i=4, t=PACK),
-                    raw_z[h][:, :, pieces[i].start - h * HALF:pieces[i].stop - h * HALF].rearrange("p t (c i) -> p c t i", i=4))
+            cols = slice(pieces[i].start - h * HALF, pieces[i].stop - h * HALF)
+            return (z_woven[i][:].rearrange("p (c n t) -> p c t n", n=LINE, t=TILES),
+                    minus_z[h][:, :, cols].rearrange("p t (c n) -> p c t n", n=LINE))
 
         def z_quantise(i):
-            nc.vector.quantize_mx(out=z_codes[:, pieces[i]].bitcast(FP8X4), scales=z_scales[:, pieces[i]], in_=z_g[i][:])
+            nc.vector.quantize_mx(out=z_codes[:, pieces[i]].bitcast(FP8X4), scales=z_scales[:, pieces[i]], in_=z_woven[i][:])
 
-        def combine(t):
+        for t in range(PAIR):
+            d_out(t)
+        for t in range(PAIR):
+            fetch_gate(t)
+        for t in range(PAIR):
+            y_out(t)
+            d_product(PAIR + t, bank=2 + t)
+            y_product(PAIR + t, bank=4 + t)
+        for t in range(PAIR):
             for h in range(2):
                 times_gate(t, h)
             for h in range(2):
-                less_neighbour(t, h)
-
-        d_out(0)
-        d_out(1)
-        gate(0)
-        gate(1)
-        y_out(0)
-        d_product(2, 2)
-        y_product(2, 4)
-        y_out(1)
-        d_product(3, 3)
-        y_product(3, 5)
-        combine(0)
-        combine(1)
-        for t in range(2, PACK):
+                neighbour_less_gated(t, h)
+        for t in range(PAIR, TILES):
             d_out(t)
             y_out(t)
-            gate(t)
+            fetch_gate(t)
             for h in range(2):
                 times_gate(t, h)
-            less_neighbour(t, 0)
-        for t in range(2, PACK):
-            less_neighbour(t, 1)
-        nc.scalar.activation(*z_views(0), ACT.Copy, scale=-0.5)
-        nc.scalar.activation(*z_views(1), ACT.Copy, scale=-0.5)
+            neighbour_less_gated(t, 0)
+        for t in range(PAIR, TILES):
+            neighbour_less_gated(t, 1)
+
+        nc.scalar.activation(*z_views(0), ACT.Copy, scale=-1.0)
+        nc.scalar.activation(*z_views(1), ACT.Copy, scale=-1.0)
         z_quantise(0)
-        nc.vector.tensor_scalar_mul(*z_views(2), -0.5)
+        nc.vector.tensor_scalar_mul(*z_views(2), -1.0)
         z_quantise(1)
         z_quantise(2)
 
-        cand_q, z_q = (cand_wd, cand_sd), (z_codes, z_scales)
         s_parts = [[(psum.tile([P, c.stop - c.start], F32, name=f"s_bank0{i}", tag=f"bank{5 + i}"), c) for i, c in enumerate(pieces)]]
-        for t in range(1, PACK):
+        for t in range(1, TILES):
             s_parts.append([(psum.tile([P, S], F32, name=f"s_bank{t}", tag=f"bank{t - 1}"), everything)])
-        for t in range(PACK):
+        for t in range(TILES):
             for bank, cols in s_parts[t]:
-                product(bank[:], cand_q, t, z_q, cols)
+                product(bank[:], (cand_words, cand_scales), t, (z_codes, z_scales), cols)
 
-        s_b = [keep.tile([P, S], F32, name=f"s_b{t}") for t in range(PACK)]
-        diff = [keep.tile([P, S], F32, name=f"diff{t}") for t in range(PACK)]
-        bent = [keep.tile([P, S], F32, name=f"bent{t}") for t in range(PACK)]
-        res = [keep.tile([P, S], F32, name=f"res{t}") for t in range(PACK)]
-        out_rows = out.rearrange("(r t q) j -> t r q j", r=RUNS, t=PACK)
+        s_plain = [keep.tile([P, S], F32, name=f"s_plain{t}") for t in range(TILES)]
+        diff = [keep.tile([P, S], F32, name=f"diff{t}") for t in range(TILES)]
+        bent = [keep.tile([P, S], F32, name=f"bent{t}") for t in range(TILES)]
+        result = [keep.tile([P, S], F32, name=f"result{t}") for t in range(TILES)]
+        out_rows = out.rearrange("(a t b) j -> t a b j", a=CAND_GROUPS, t=TILES)
 
-        def s_out(t):
+        def difference(t):
             for bank, cols in s_parts[t]:
-                nc.scalar.activation(wide_s[t][:, cols], bank[:], ACT.Copy, scale=0.0625)
+                nc.scalar.activation(windows[t][:, cols], bank[:], ACT.Copy, scale=0.0625)
             for bank, cols in s_parts[t]:
                 if cols == pieces[0]:
-                    nc.vector.tensor_scalar_mul(s_b[t][:, cols], bank[:], 0.0625)
+                    nc.vector.tensor_scalar_mul(s_plain[t][:, cols], bank[:], 0.0625)
                 else:
-                    nc.scalar.activation(s_b[t][:, cols], bank[:], ACT.Copy, scale=0.0625)
+                    nc.scalar.activation(s_plain[t][:, cols], bank[:], ACT.Copy, scale=0.0625)
             for cols in (halves if t == 0 else [everything]):
-                nc.vector.tensor_tensor(diff[t][:, cols], wide_s[t][:].indirect(part(n3_l, cols)), s_b[t][:, cols], ALU.subtract)
+                nc.vector.tensor_tensor(diff[t][:, cols], windows[t][:].indirect(entries(n3_l, cols)), s_plain[t][:, cols], ALU.subtract)
 
         def finish(t):
             nc.scalar.activation(bent[t][:], diff[t][:], ACT.Tanh)
-            for cols in ([slice(0, S - P), slice(S - P, S)] if t == PACK - 1 else [everything]):
-                nc.vector.tensor_tensor(res[t][:, cols], wide_s[t][:].indirect(part(n4_l, cols)), bent[t][:, cols], ALU.mult)
-                nc.sync.dma_start(out_rows[t][:, :, cols], res[t][:, cols])
+            for cols in ([slice(0, S - P), slice(S - P, S)] if t == TILES - 1 else [everything]):
+                nc.vector.tensor_tensor(result[t][:, cols], windows[t][:].indirect(entries(n4_l, cols)), bent[t][:, cols], ALU.mult)
+                nc.sync.dma_start(out_rows[t][:, :, cols], result[t][:, cols])
 
-        s_out(0)
-        for t in range(1, PACK):
-            s_out(t)
+        difference(0)
+        for t in range(1, TILES):
+            difference(t)
             finish(t - 1)
-        finish(PACK - 1)
+        finish(TILES - 1)

import concourse.mybir as mybir

F32 = mybir.dt.float32
BF16 = mybir.dt.bfloat16
I32 = mybir.dt.int32
U32 = mybir.dt.uint32
U16 = mybir.dt.uint16
U8 = mybir.dt.uint8
FP8X4 = mybir.dt.float8_e4m3fn_x4
ACT = mybir.ActivationFunctionType
ALU = mybir.AluOpType

P = 128
T = 2048
S = 512
H = 512
C = 512
PACK = 4
TILES = 4
PAIR = 2
HALF = S // 2
LIST_ROWS = 16
CAND_GROUPS = 16
LINE = 4
ALIGN = 64
FLOPS = 3 * 2 * 512 * 512 * 512

W1_WOVEN_AT = (0, 2048)
W2_CODES_AT, W2_SCALES_AT, CAND_DEALT_AT, CAND_BYTES_AT = 0, 1024, 1280, 1792
CAND_WORDS_AT = 2048
MINUS_Z_AT = (4096, 8192)
Z_WOVEN_AT = (12288, 14336, MINUS_Z_AT[0])


def tile_picked_twcgatebfdif_none_p_kernel(tc, x_words, x_scales, w1, w2, gs, offs, two, n1, n2, cand, n3, n4, out):
    nc = tc.nc
    with (
        tc.tile_pool(name="keep", bufs=1) as keep,
        tc.tile_pool(name="reused", bufs=1) as reused,
        tc.psum_pool(name="psum", bufs=1) as psum,
    ):
        def load_list(src, name):
            tile = keep.tile([P, S // LIST_ROWS], U16, name=name)
            nc.sync.dma_start(tile[:], src)
            return tile

        def entries(lst, cols):
            return lst[:, cols.start // LIST_ROWS:cols.stop // LIST_ROWS]

        def weave(engine_copy, woven, raw, u):
            engine_copy(woven[:].rearrange("p (t m j) -> p m j t", t=PAIR, j=PACK),
                        raw[:].rearrange("p (j m t) -> p m j t", j=PACK, t=TILES)[:, :, :, PAIR * u:PAIR * (u + 1)])

        def quantise(woven, codes, scales):
            nc.vector.quantize_mx(out=codes[:].bitcast(FP8X4), scales=scales[:], in_=woven[:])
            return codes, scales

        def weight_tiles(name):
            return (keep.tile([P, PAIR * P], U32, name=f"{name}_codes", align_bytes=ALIGN),
                    keep.tile([P, PAIR * P], U8, name=f"{name}_scales", align_bytes=ALIGN))

        def pick(window, offsets, picked):
            nc.vector.tensor_copy(picked[:], window.indirect(offsets))
            return picked

        def product(bank, lhs, block, rhs, cols):
            m = slice(block * P, (block + 1) * P)
            nc.tensor.matmul_mx(out=bank, lhsT=lhs[0][:, m].bitcast(FP8X4), lhsT_scale=lhs[1][:, m],
                                rhs=rhs[0][:, cols].bitcast(FP8X4), rhs_scale=rhs[1][:, cols], start=True, stop=True)

        xs = keep.tile([P, T], U8, name="xs")
        nc.vector.memset(xs[:].bitcast(I32), 0)
        one_half = keep.tile([P, 8], F32, name="one_half")
        nc.gpsimd.memset(one_half[:], 0.0)
        nc.scalar.activation(one_half[:], one_half[:], ACT.Sigmoid)
        cleared = [keep.tile([P, 2 * S], F32, name=f"cleared{t}") for t in range(PAIR)]
        for tile in cleared:
            nc.gpsimd.memset(tile[:, S:], 0.0)

        two_l = load_list(two, "two_l")
        offs_l = load_list(offs, "offs_l")
        w2_raw = keep.tile([P, PACK * H], F32, name="w2_raw")
        w2_rows = w2.rearrange("(p j) c -> p (j c)", j=PACK)
        nc.sync.dma_start(w2_raw[:, :2 * H], w2_rows[:, :2 * H])
        for q in range(4):
            nc.sync.dma_start(xs[32 * q:32 * q + 4, :].bitcast(I32), x_scales[0, 4 * q:4 * q + 4, :].bitcast(I32))
        nc.sync.dma_start(w2_raw[:, 2 * H:], w2_rows[:, 2 * H:])
        cand_l = load_list(cand, "cand_l")
        xw = keep.tile([P, T], I32, name="xw")
        nc.sync.dma_start(xw[:], x_words[0].rearrange("p n r -> p (n r)").bitcast(I32))
        gain = keep.tile([P, TILES], F32, name="gain")
        nc.sync.dma_start(gain[:], gs.rearrange("(p t) o -> p (t o)", t=TILES))
        n2_l = load_list(n2, "n2_l")
        w1_raw = keep.tile([P, PACK * H], F32, name="w1_raw")
        nc.sync.dma_start(w1_raw[:], w1.rearrange("(p j) c -> p (j c)", j=PACK))
        n1_l = load_list(n1, "n1_l")
        n3_l = load_list(n3, "n3_l")
        n4_l = load_list(n4, "n4_l")

        halves = [slice(0, HALF), slice(HALF, S)]
        everything = slice(0, S)
        words = xw[:].bitcast(U32)
        two_s = pick(xs[:], two_l[:], keep.tile([P, S], U8, name="two_s", align_bytes=ALIGN))
        offs_s = pick(xs[:], offs_l[:], keep.tile([P, S], U8, name="offs_s", align_bytes=ALIGN))
        cand_s = [pick(xs[:], entries(cand_l, halves[0]), keep.tile([P, C // 2], U8, name="cand_s0", align_bytes=ALIGN))]
        w2_woven = [keep.tile([P, PAIR * P * PACK], BF16, name=f"w2_woven{u}", align_bytes=ALIGN) for u in range(2)]
        for u in range(2):
            weave(nc.scalar.copy, w2_woven[u], w2_raw, u)
        w2_q = [quantise(w2_woven[0], *weight_tiles("w2_q0"))]
        two_w = pick(words, two_l[:], keep.tile([P, S], U32, name="two_w", align_bytes=ALIGN))
        offs_w = pick(words, offs_l[:], keep.tile([P, S], U32, name="offs_w", align_bytes=ALIGN))
        half_gain = keep.tile([P, TILES], F32, name="half_gain")
        nc.scalar.activation(half_gain[:], gain[:], ACT.Copy, scale=one_half[:, 0:1])

        d_banks, y_banks = {}, {}

        def d_product(t, bank):
            d_banks[t] = psum.tile([P, S], F32, name=f"d_bank{t}", tag=f"bank{bank}")
            product(d_banks[t][:], w2_q[t // PAIR], t % PAIR, (two_w, two_s), everything)

        def y_product(t, bank):
            y_banks[t] = psum.tile([P, S], F32, name=f"y_bank{t}", tag=f"bank{bank}")
            product(y_banks[t][:], w1_q[t // PAIR], t % PAIR, (offs_w, offs_s), everything)

        d_product(0, bank=0)
        d_product(1, bank=1)

        w1_woven = [reused.tile([P, PAIR * P * PACK], BF16, name=f"w1_woven{u}", align_bytes=ALIGN, offset=W1_WOVEN_AT[u])
                    for u in range(2)]
        for u in range(2):
            weave(nc.vector.tensor_copy, w1_woven[u], w1_raw, u)
        w1_q = [quantise(w1_woven[u], *weight_tiles(f"w1_q{u}")) for u in range(2)]
        y_product(0, bank=2)
        y_product(1, bank=3)

        w2_q.append(quantise(w2_woven[1],
                             reused.tile([P, PAIR * P], U32, name="w2_q1_codes", align_bytes=ALIGN, offset=W2_CODES_AT),
                             reused.tile([P, PAIR * P], U8, name="w2_q1_scales", align_bytes=ALIGN, offset=W2_SCALES_AT)))
        cand_s.append(pick(xs[:], entries(cand_l, halves[1]),
                           reused.tile([P, C // 2], U8, name="cand_s1", align_bytes=ALIGN, offset=CAND_BYTES_AT)))
        cand_words = reused.tile([P, C], U32, name="cand_words", align_bytes=ALIGN, offset=CAND_WORDS_AT)
        nc.vector.tensor_copy(cand_words[:].rearrange("p (t a b) -> p a t b", t=TILES, a=CAND_GROUPS), words.indirect(cand_l[:]))
        cand_scales = reused.tile([P, C], U8, name="cand_scales", align_bytes=ALIGN, offset=CAND_DEALT_AT)
        dealt = cand_scales[:].bitcast(I32).rearrange("p (t a w) -> p a t w", t=TILES, a=CAND_GROUPS)
        for h in range(2):
            nc.vector.tensor_copy(dealt[:, h * CAND_GROUPS // 2:(h + 1) * CAND_GROUPS // 2],
                                  cand_s[h][:].bitcast(I32).rearrange("p (a t w) -> p a t w", t=TILES, a=CAND_GROUPS // 2))

        windows = cleared + [w2_raw, w1_raw]
        gate = [keep.tile([P, S], F32, name=f"gate{t}") for t in range(TILES)]
        half_y = [keep.tile([P, S], F32, name=f"half_y{t}") for t in range(TILES)]
        minus_z = [reused.tile([P, TILES, HALF], F32, name=f"minus_z{h}", align_bytes=ALIGN, offset=MINUS_Z_AT[h])
                   for h in range(2)]
        gated = [[windows[t][:, S + h * HALF:S + (h + 1) * HALF] for h in range(2)] for t in range(TILES)]
        gated[3][0] = minus_z[1][:, 2, :]
        z_codes = keep.tile([P, S], U32, name="z_codes", align_bytes=ALIGN)
        z_scales = keep.tile([P, S], U8, name="z_scales", align_bytes=ALIGN)
        pieces = [halves[0], slice(HALF, HALF + P), slice(HALF + P, S)]
        z_woven = [reused.tile([P, (c.stop - c.start) * PACK], BF16, name=f"z_woven{i}", align_bytes=ALIGN, offset=Z_WOVEN_AT[i])
                   for i, c in enumerate(pieces)]

        def d_out(t):
            nc.scalar.copy(windows[t][:, :S], d_banks[t][:])

        def y_out(t):
            nc.scalar.activation(half_y[t][:], y_banks[t][:], ACT.Copy, scale=half_gain[:, t:t + 1])

        def fetch_gate(t):
            nc.scalar.activation(gate[t][:], windows[t][:].indirect(n2_l[:]), ACT.Sigmoid)

        def times_gate(t, h):
            nc.vector.scalar_tensor_tensor(gated[t][h], half_y[t][:, halves[h]], 2.0, gate[t][:, halves[h]], ALU.mult, ALU.mult)

        def neighbour_less_gated(t, h):
            nc.vector.tensor_tensor(minus_z[h][:, t, :], half_y[t][:].indirect(entries(n1_l, halves[h])), gated[t][h], ALU.subtract)

        def z_views(i):
            h = pieces[i].start // HALF
            cols = slice(pieces[i].start - h * HALF, pieces[i].stop - h * HALF)
            return (z_woven[i][:].rearrange("p (c n t) -> p c t n", n=LINE, t=TILES),
                    minus_z[h][:, :, cols].rearrange("p t (c n) -> p c t n", n=LINE))

        def z_quantise(i):
            nc.vector.quantize_mx(out=z_codes[:, pieces[i]].bitcast(FP8X4), scales=z_scales[:, pieces[i]], in_=z_woven[i][:])

        for t in range(PAIR):
            d_out(t)
        for t in range(PAIR):
            fetch_gate(t)
        for t in range(PAIR):
            y_out(t)
            d_product(PAIR + t, bank=2 + t)
            y_product(PAIR + t, bank=4 + t)
        for t in range(PAIR):
            for h in range(2):
                times_gate(t, h)
            for h in range(2):
                neighbour_less_gated(t, h)
        for t in range(PAIR, TILES):
            d_out(t)
            y_out(t)
            fetch_gate(t)
            for h in range(2):
                times_gate(t, h)
            neighbour_less_gated(t, 0)
        for t in range(PAIR, TILES):
            neighbour_less_gated(t, 1)

        nc.scalar.activation(*z_views(0), ACT.Copy, scale=-1.0)
        nc.scalar.activation(*z_views(1), ACT.Copy, scale=-1.0)
        z_quantise(0)
        nc.vector.tensor_scalar_mul(*z_views(2), -1.0)
        z_quantise(1)
        z_quantise(2)

        s_parts = [[(psum.tile([P, c.stop - c.start], F32, name=f"s_bank0{i}", tag=f"bank{5 + i}"), c) for i, c in enumerate(pieces)]]
        for t in range(1, TILES):
            s_parts.append([(psum.tile([P, S], F32, name=f"s_bank{t}", tag=f"bank{t - 1}"), everything)])
        for t in range(TILES):
            for bank, cols in s_parts[t]:
                product(bank[:], (cand_words, cand_scales), t, (z_codes, z_scales), cols)

        s_plain = [keep.tile([P, S], F32, name=f"s_plain{t}") for t in range(TILES)]
        diff = [keep.tile([P, S], F32, name=f"diff{t}") for t in range(TILES)]
        bent = [keep.tile([P, S], F32, name=f"bent{t}") for t in range(TILES)]
        result = [keep.tile([P, S], F32, name=f"result{t}") for t in range(TILES)]
        out_rows = out.rearrange("(a t b) j -> t a b j", a=CAND_GROUPS, t=TILES)

        def difference(t):
            for bank, cols in s_parts[t]:
                nc.scalar.activation(windows[t][:, cols], bank[:], ACT.Copy, scale=0.0625)
            for bank, cols in s_parts[t]:
                if cols == pieces[0]:
                    nc.vector.tensor_scalar_mul(s_plain[t][:, cols], bank[:], 0.0625)
                else:
                    nc.scalar.activation(s_plain[t][:, cols], bank[:], ACT.Copy, scale=0.0625)
            for cols in (halves if t == 0 else [everything]):
                nc.vector.tensor_tensor(diff[t][:, cols], windows[t][:].indirect(entries(n3_l, cols)), s_plain[t][:, cols], ALU.subtract)

        def finish(t):
            nc.scalar.activation(bent[t][:], diff[t][:], ACT.Tanh)
            for cols in ([slice(0, S - P), slice(S - P, S)] if t == TILES - 1 else [everything]):
                nc.vector.tensor_tensor(result[t][:, cols], windows[t][:].indirect(entries(n4_l, cols)), bent[t][:, cols], ALU.mult)
                nc.sync.dma_start(out_rows[t][:, :, cols], result[t][:, cols])

        difference(0)
        for t in range(1, TILES):
            difference(t)
            finish(t - 1)
        finish(TILES - 1)
